import numpy as np
import ml_dtypes


def mxq(x, axis, fmt="e4m3"):
    dtype, down = {"e4m3": (ml_dtypes.float8_e4m3fn, 7), "e5m2": (ml_dtypes.float8_e5m2, 14)}[fmt]
    v = np.moveaxis(np.asarray(x, np.float32).astype(ml_dtypes.bfloat16).astype(np.float64), axis, -1)
    blocks = v.reshape(v.shape[:-1] + (-1, 32))
    amax = np.abs(blocks).max(-1, keepdims=True)
    byte = np.maximum(np.where(amax > 0, np.frexp(amax)[1] - 1 + 127, 0) - down, 1)
    scale = np.exp2(byte - 127.0)
    codes = (blocks / scale).astype(np.float32).astype(dtype).astype(np.float64)
    return np.moveaxis((codes * scale).reshape(v.shape), -1, axis)


WIDE = False


def mx_kscale(k):
    if not WIDE:
        return np.ones(k)
    levels = np.array([10, -10, 5, -5, 0])
    if k % 512:
        return np.exp2(np.random.permutation(np.resize(levels, k // 32))).repeat(32)
    a = np.empty((k // 512, 16))
    for p in range(k // 512):
        a[p, :8] = np.random.permutation(np.resize(levels, 8))
        for g in range(8):
            far = levels[np.abs(levels - a[p, g]) >= 10]
            a[p, g + 8] = far[np.random.randint(len(far))]
    return np.exp2(a.ravel()).repeat(32)


def f64(x):
    return np.asarray(x).astype(np.float64)


def striped(idx):
    return np.tile(idx.reshape(-1, 16).T, (8, 1)).astype(np.uint16)


def unstriped(offs):
    return offs[:16].T.reshape(-1).astype(np.int64)


def striped8(idx):
    return np.concatenate([x.reshape(-1, 16).T for x in idx]).astype(np.uint16)


def runs(offs, k):
    lists = np.stack([offs[16 * r : 16 * r + 16].T.reshape(-1) for r in range(8)]).astype(np.int64)
    return lists[np.arange(k) % 512 // 64]


def pack_weight(w):
    k, n = w.shape
    w = f64(np.asarray(w, np.float32).astype(ml_dtypes.bfloat16)).reshape(k // 32, 32, n)
    amax = np.abs(w).max(1)
    byte = np.clip(np.where(amax > 0, np.frexp(amax)[1] - 1 + 127 - 7, 1), 1, 254)
    scaled = (w * np.exp2(127.0 - byte)[:, None, :]).reshape(k, n).astype(np.float32)
    words = np.ascontiguousarray(scaled.reshape(k // 512, 128, 4, n).transpose(0, 1, 3, 2)).astype(ml_dtypes.float8_e4m3fn).view(np.uint8)
    return words, np.ascontiguousarray(byte.astype(np.uint8).reshape(k // 512, 16, n))


def unpack_weight(words, scales):
    g, p, n, _ = words.shape
    vals = np.ascontiguousarray(words).view(ml_dtypes.float8_e4m3fn).astype(np.float64) * np.repeat(np.exp2(scales.astype(np.float64) - 127.0), 8, axis=1)[..., None]
    return vals.transpose(0, 1, 3, 2).reshape(g * 512, n)


E2M1 = np.array([0.0, 0.5, 1.0, 1.5, 2.0, 3.0, 4.0, 6.0, -0.0, -0.5, -1.0, -1.5, -2.0, -3.0, -4.0, -6.0])


def pack_fp4(w):
    k, n = w.shape
    w = f64(np.asarray(w, np.float32).astype(ml_dtypes.bfloat16)).reshape(k // 32, 32, n)
    amax = np.abs(w).max(1)
    mant, ex = np.frexp(amax / 6.0)
    byte = np.clip(np.where(amax > 0, np.where(mant > 0.5, ex, ex - 1) + 127, 1), 1, 254)
    scaled = (w * np.exp2(127.0 - byte)[:, None, :]).reshape(k, n).astype(np.float32)
    c = np.ascontiguousarray(scaled.reshape(k // 512, 128, 4, n).transpose(0, 1, 3, 2)).astype(ml_dtypes.float4_e2m1fn).view(np.uint8) & 0xF
    words = (c[..., 0::2] | (c[..., 1::2] << 4)).reshape(k // 512, 128, 2 * n)
    return np.ascontiguousarray(words), np.ascontiguousarray(byte.astype(np.uint8).reshape(k // 512, 16, n))


def unpack_fp4(words, scales):
    g, _, n = scales.shape
    words = np.ascontiguousarray(words).reshape(g, 128, n, 2)
    nib = np.empty((g, 128, n, 4), np.uint8)
    nib[..., 0::2] = words & 0xF
    nib[..., 1::2] = words >> 4
    vals = E2M1[nib] * np.repeat(np.exp2(scales.astype(np.float64) - 127.0), 8, axis=1)[..., None]
    return vals.transpose(0, 1, 3, 2).reshape(g * 512, n)


def sigmoid(v):
    return 1.0 / (1.0 + np.exp(-np.maximum(v, -700.0)))

def planes(y):
    n, m = y.shape
    v = y.astype(np.float32).astype(ml_dtypes.bfloat16).astype(np.float64).reshape(n // 32, 32, m)
    top = np.abs(v).max(1)
    byte = np.clip(np.where(top > 0, np.frexp(top)[1] - 1 + 127 - 7, 1), 1, 254)
    codes = (v * np.exp2(127.0 - byte)[:, None, :]).reshape(n, m).astype(np.float32).astype(ml_dtypes.float8_e4m3fn).view(np.uint8)
    words = codes.reshape(n // 512, 128, 4, m).transpose(0, 1, 3, 2)
    return np.ascontiguousarray(words), np.ascontiguousarray(byte.astype(np.uint8).reshape(n // 512, 16, m))


K, T, S, V, N, U, H = 512, 2048, 512, 1024, 512, 1024, 512


def setup_inputs():
    n = np.random.standard_normal
    s = mx_kscale(K)[:, None]
    u = mx_kscale(H)
    packed_xT = pack_weight(n((K, T)) * s)
    packed_w2 = pack_fp4(n((K, H)) / np.sqrt(K) / s)
    packed_w3 = pack_fp4(n((H, N)) / np.sqrt(H) / u[:, None])
    return {
        "x_words": packed_xT[0],
        "x_scales": packed_xT[1],
        "w1": (n((K, H)) / np.sqrt(K) / s * u).astype(np.float32),
        "w2_words": packed_w2[0],
        "w2_scales": packed_w2[1],
        "ma": (n((H, U)) * u[:, None]).astype(np.float32),
        "mb": n((H, U)).astype(np.float32),
        "w3_words": packed_w3[0],
        "w3_scales": packed_w3[1],
        "offs": striped(np.random.permutation(T)[:S]),
        "two": striped(np.random.permutation(T)[:S]),
        "s1": striped8(np.stack([np.random.permutation(U)[:S] for _ in range(8)])),
        "s2": striped8(np.stack([np.random.permutation(U)[:S] for _ in range(8)])),
        "r1": striped8(np.stack([np.random.permutation(U) for _ in range(8)])),
        "r2": striped8(np.stack([np.random.permutation(U) for _ in range(8)])),
    }


def reference(x_words, x_scales, w1, w2_words, w2_scales, ma, mb, w3_words, w3_scales, offs, two, s1, s2, r1, r2):
    xq = unpack_weight(x_words, x_scales)[:, unstriped(offs)]
    y = mxq(f64(w1), 0, "e4m3").T @ xq
    pa = f64(ma).copy()
    pa[np.arange(H)[:, None], runs(s1, H)] = y
    x_two = unpack_weight(x_words, x_scales)[:, unstriped(two)]
    e = unpack_fp4(w2_words, w2_scales).T @ x_two
    pb = f64(mb).copy()
    pb[np.arange(H)[:, None], runs(s2, H)] = e
    z = (pa[np.arange(H)[:, None], runs(r1, H)]) * (sigmoid(pb[np.arange(H)[:, None], runs(r2, H)]))
    out_0 = unpack_fp4(w3_words, w3_scales).T @ mxq(z, 0, "e4m3")
    return (out_0,) + planes(out_0)

@@ -1,0 +1,216 @@
+from contextlib import ExitStack
+
+import concourse.mybir as mybir
+
+K, T, S, V, N, U, H = 512, 2048, 512, 1024, 512, 1024, 512
+FLOPS = 2 * K * H * S * 2 + 2 * H * N * V
+
+F32 = mybir.dt.float32
+BF16 = mybir.dt.bfloat16
+I32 = mybir.dt.int32
+U32 = mybir.dt.uint32
+U16 = mybir.dt.uint16
+U8 = mybir.dt.uint8
+FP8X4 = mybir.dt.float8_e4m3fn_x4
+FP4X4 = mybir.dt.float4_e2m1fn_x4
+ACT = mybir.ActivationFunctionType
+MULT = mybir.AluOpType.mult
+
+P = 128
+PACK = 4
+CH = 256
+NCH = V // CH
+
+
+def tile_picked_twopage_none_po_kernel(
+    tc, x_words, x_scales, w1, w2_words, w2_scales, ma, mb, w3_words, w3_scales,
+    offs, two, s1, s2, r1, r2, out_0, out_1, out_2,
+):
+    nc = tc.nc
+    with ExitStack() as ctx:
+        keep = ctx.enter_context(tc.tile_pool(name="keep", bufs=1))
+        psum = ctx.enter_context(tc.psum_pool(name="psum", bufs=8))
+
+        def sb(shape, dtype, name):
+            return keep.tile(shape, dtype, name=name, align_bytes=64)
+
+        def load_list(src, name):
+            t = sb([P, src.shape[1]], U16, name)
+            nc.sync.dma_start(t[:], src)
+            return t
+
+        def load_scale_rows(tile, src):
+            for q in range(4):
+                nc.sync.dma_start(
+                    out=tile[32 * q : 32 * q + 4, :].bitcast(I32),
+                    in_=src[0, 4 * q : 4 * q + 4, :].bitcast(I32),
+                )
+
+        def load_page(src, t, name):
+            page = sb([P, U], F32, name)
+            nc.sync.dma_start(out=page[:], in_=src.rearrange("(p t) u -> p t u", t=PACK)[:, t, :])
+            return page
+
+        xs = sb([P, T], U8, "xs")
+        w2s_raw = sb([P, H], U8, "w2s_raw")
+        w3s_raw = sb([P, N], U8, "w3s_raw")
+        nc.vector.memset(xs[:].bitcast(I32), 0)
+        nc.vector.memset(w2s_raw[:].bitcast(I32), 0)
+        nc.vector.memset(w3s_raw[:].bitcast(I32), 0)
+
+        two_t = load_list(two, "two_t")
+        load_scale_rows(xs, x_scales)
+        offs_t = load_list(offs, "offs_t")
+        xw = sb([P, T], U32, "xw")
+        nc.sync.dma_start(out=xw[:].bitcast(I32), in_=x_words[0].rearrange("p c r -> p (c r)").bitcast(I32))
+        w2w_raw = sb([P, 2 * H], U8, "w2w_raw")
+        nc.sync.dma_start(out=w2w_raw[:].bitcast(I32), in_=w2_words[0].bitcast(I32))
+        load_scale_rows(w2s_raw, w2_scales)
+        s2_t = load_list(s2, "s2_t")
+        pb = [load_page(mb, 0, "pb0")]
+        w1_raw = sb([P, PACK, H], F32, "w1_raw")
+        nc.sync.dma_start(out=w1_raw[:], in_=w1.rearrange("(p j) c -> p j c", j=PACK))
+        r2_t = load_list(r2, "r2_t")
+        s1_t = load_list(s1, "s1_t")
+        r1_t = load_list(r1, "r1_t")
+        for t in range(1, PACK):
+            pb.append(load_page(mb, t, "pb%d" % t))
+        pa = [load_page(ma, t, "pa%d" % t) for t in range(PACK)]
+        w3w_raw = sb([P, 2 * N], U8, "w3w_raw")
+        nc.sync.dma_start(out=w3w_raw[:].bitcast(I32), in_=w3_words[0].bitcast(I32))
+        load_scale_rows(w3s_raw, w3_scales)
+
+        def gather(window, lst, dtype, name):
+            got = sb([P, S], dtype, name)
+            nc.vector.tensor_copy(got[:], window[:].indirect(lst[:]))
+            return got
+
+        def deal_words(raw, name):
+            dealt = sb([P, 2 * H], U8, name)
+            nc.scalar.copy(
+                out=dealt[:].bitcast(U16).rearrange("p (t m) -> p m t", t=PACK),
+                in_=raw[:].bitcast(U16).rearrange("p (m t) -> p m t", t=PACK),
+            )
+            return dealt
+
+        def deal_scales(raw, name):
+            dealt = sb([P, H], U8, name)
+            nc.vector.tensor_copy(
+                out=dealt[:].rearrange("p (t m) -> p t m", t=PACK),
+                in_=raw[:].rearrange("p (m t) -> p t m", t=PACK),
+            )
+            return dealt
+
+        x2s = gather(xs, two_t, U8, "x2s")
+        x2w = gather(xw, two_t, U32, "x2w")
+        w2w = deal_words(w2w_raw, "w2w")
+        w2s = deal_scales(w2s_raw, "w2s")
+        x1w = gather(xw, offs_t, U32, "x1w")
+        x1s = gather(xs, offs_t, U8, "x1s")
+
+        def product(lhsT, lhsT_scale, xw_t, xs_t, name):
+            acc = psum.tile([P, S], F32, name="acc")
+            nc.tensor.matmul_mx(
+                out=acc[:], lhsT=lhsT, lhsT_scale=lhsT_scale,
+                rhs=xw_t[:].bitcast(FP8X4), rhs_scale=xs_t[:], start=True, stop=True,
+            )
+            res = sb([P, S], F32, name)
+            nc.scalar.copy(out=res[:], in_=acc[:])
+            return res
+
+        e = [
+            product(w2w[:, 2 * P * t : 2 * P * (t + 1)].bitcast(FP4X4), w2s[:, P * t : P * (t + 1)], x2w, x2s, "e%d" % t)
+            for t in range(PACK)
+        ]
+
+        w1b = sb([P, PACK * H], BF16, "w1b")
+        nc.scalar.copy(
+            out=w1b[:].rearrange("p (t m j) -> p m j t", t=PACK, j=PACK),
+            in_=w1_raw[:].rearrange("p j (m t) -> p m j t", t=PACK),
+        )
+        w1w = sb([P, H], U32, "w1w")
+        w1s = sb([P, H], U8, "w1s")
+        nc.vector.tensor_copy(pb[0][:].indirect(s2_t[:]), e[0][:])
+        nc.vector.quantize_mx(out=w1w[:].bitcast(FP8X4), scales=w1s[:], in_=w1b[:])
+        y = [
+            product(w1w[:, P * t : P * (t + 1)].bitcast(FP8X4), w1s[:, P * t : P * (t + 1)], x1w, x1s, "y%d" % t)
+            for t in range(PACK)
+        ]
+        w3w = deal_words(w3w_raw, "w3w")
+
+        gate = [sb([P, PACK, CH], F32, "gate%d" % c) for c in range(NCH)]
+        read = [sb([P, PACK, CH], F32, "read%d" % c) for c in range(NCH)]
+
+        def fetch(dst, page, lst, t, func):
+            for c in range(NCH):
+                cols = slice(c * CH // 16, (c + 1) * CH // 16)
+                nc.scalar.activation(out=dst[c][:, t, :], in_=page[:].indirect(lst[:, cols]), func=func)
+
+        for t in range(PACK):
+            if t > 0:
+                nc.vector.tensor_copy(pb[t][:].indirect(s2_t[:]), e[t][:])
+            fetch(gate, pb[t], r2_t, t, ACT.Sigmoid)
+        for t in range(PACK):
+            nc.vector.tensor_copy(pa[t][:].indirect(s1_t[:]), y[t][:])
+            fetch(read, pa[t], r1_t, t, ACT.Copy)
+        w3s = deal_scales(w3s_raw, "w3s")
+
+        zb = [sb([P, PACK * CH], BF16, "zb%d" % c) for c in range(NCH)]
+        zw = [sb([P, CH], U32, "zw%d" % c) for c in range(NCH)]
+        zs = [sb([P, CH], U8, "zs%d" % c) for c in range(NCH)]
+        of = [sb([P, PACK, CH], F32, "of%d" % c) for c in range(NCH)]
+        ob = [sb([P, PACK * CH], BF16, "ob%d" % c) for c in range(NCH)]
+        ow = [sb([P, CH], U32, "ow%d" % c) for c in range(NCH)]
+        osc = sb([P, V], U8, "osc")
+        out_rows = out_0.rearrange("(p t) v -> p t v", t=PACK)
+        out_words = out_1[0].rearrange("p c r -> p (c r)").bitcast(I32)
+
+        def planes(ap):
+            return ap.rearrange("p t (c i) -> p c t i", i=4)
+
+        def woven(ap):
+            return ap.rearrange("p (c i t) -> p c t i", i=4, t=PACK)
+
+        def mult(c):
+            nc.vector.tensor_tensor(woven(zb[c][:]), planes(read[c][:]), planes(gate[c][:]), MULT)
+
+        def quant_z(c):
+            nc.vector.quantize_mx(out=zw[c][:].bitcast(FP8X4), scales=zs[c][:], in_=zb[c][:])
+
+        def last_product(c):
+            for h in range(2):
+                acc = psum.tile([P, S], F32, name="acc")
+                for u in range(2):
+                    t = 2 * h + u
+                    nc.tensor.matmul_mx(
+                        out=acc[:, u * CH : (u + 1) * CH],
+                        lhsT=w3w[:, 2 * P * t : 2 * P * (t + 1)].bitcast(FP4X4),
+                        lhsT_scale=w3s[:, P * t : P * (t + 1)],
+                        rhs=zw[c][:].bitcast(FP8X4), rhs_scale=zs[c][:], start=True, stop=True,
+                    )
+                nc.scalar.copy(out=of[c][:, 2 * h : 2 * h + 2, :].rearrange("p t c -> p (t c)"), in_=acc[:])
+            nc.sync.dma_start(out=out_rows[:, :, c * CH : (c + 1) * CH], in_=of[c][:])
+
+        def round_out(c):
+            nc.vector.tensor_copy(out=woven(ob[c][:]), in_=planes(of[c][:]))
+
+        def quant_out(c):
+            cols = slice(c * CH, (c + 1) * CH)
+            nc.vector.quantize_mx(out=ow[c][:].bitcast(FP8X4), scales=osc[:, cols], in_=ob[c][:])
+            nc.sync.dma_start(out=out_words[:, cols], in_=ow[c][:].bitcast(I32))
+
+        for step in range(NCH + 3):
+            if step < NCH:
+                mult(step)
+            if 1 <= step <= NCH:
+                quant_z(step - 1)
+                last_product(step - 1)
+            if 3 <= step:
+                quant_out(step - 3)
+            if 2 <= step < NCH + 2:
+                round_out(step - 2)
+        for q in range(4):
+            nc.sync.dma_start(
+                out=out_2[0, 4 * q : 4 * q + 4, :].bitcast(I32),
+                in_=osc[32 * q : 32 * q + 4, :].bitcast(I32),
+            )

@@ -18,8 +18,10 @@ MULT = mybir.AluOpType.mult
 
 P = 128
 PACK = 4
-CH = 256
+CH = 512
 NCH = V // CH
+WIDTHS = (128, 128, 256, 256, 256)
+ROUND_ON_SCALAR = (0, 1)
 
 
 def tile_picked_twopage_none_po_kernel(
@@ -31,17 +33,17 @@ def tile_picked_twopage_none_po_kernel(
         keep = ctx.enter_context(tc.tile_pool(name="keep", bufs=1))
         psum = ctx.enter_context(tc.psum_pool(name="psum", bufs=8))
 
-        def sb(shape, dtype, name):
-            return keep.tile(shape, dtype, name=name, align_bytes=64)
+        def sb(shape, dtype, name, tag=""):
+            return keep.tile(shape, dtype, name=name, tag=tag or name, align_bytes=64)
 
         def load_list(src, name):
             t = sb([P, src.shape[1]], U16, name)
             nc.sync.dma_start(t[:], src)
             return t
 
-        def load_scale_rows(tile, src):
+        def load_scale_rows(tile, src, queues):
             for q in range(4):
-                nc.sync.dma_start(
+                queues[q].dma_start(
                     out=tile[32 * q : 32 * q + 4, :].bitcast(I32),
                     in_=src[0, 4 * q : 4 * q + 4, :].bitcast(I32),
                 )
@@ -59,13 +61,15 @@ def tile_picked_twopage_none_po_kernel(
         nc.vector.memset(w3s_raw[:].bitcast(I32), 0)
 
         two_t = load_list(two, "two_t")
-        load_scale_rows(xs, x_scales)
         offs_t = load_list(offs, "offs_t")
-        xw = sb([P, T], U32, "xw")
-        nc.sync.dma_start(out=xw[:].bitcast(I32), in_=x_words[0].rearrange("p c r -> p (c r)").bitcast(I32))
         w2w_raw = sb([P, 2 * H], U8, "w2w_raw")
         nc.sync.dma_start(out=w2w_raw[:].bitcast(I32), in_=w2_words[0].bitcast(I32))
-        load_scale_rows(w2s_raw, w2_scales)
+        load_scale_rows(xs, x_scales, [nc.sync] * 4)
+        xw = sb([P, T], U32, "xw")
+        nc.sync.dma_start(out=xw[:].bitcast(I32), in_=x_words[0].rearrange("p c r -> p (c r)").bitcast(I32))
+        load_scale_rows(w2s_raw, w2_scales, [nc.sync] * 4)
+        w3w_raw = sb([P, 2 * N], U8, "w3w_raw")
+        nc.sync.dma_start(out=w3w_raw[:].bitcast(I32), in_=w3_words[0].bitcast(I32))
         s2_t = load_list(s2, "s2_t")
         pb = [load_page(mb, 0, "pb0")]
         w1_raw = sb([P, PACK, H], F32, "w1_raw")
@@ -76,12 +80,10 @@ def tile_picked_twopage_none_po_kernel(
         for t in range(1, PACK):
             pb.append(load_page(mb, t, "pb%d" % t))
         pa = [load_page(ma, t, "pa%d" % t) for t in range(PACK)]
-        w3w_raw = sb([P, 2 * N], U8, "w3w_raw")
-        nc.sync.dma_start(out=w3w_raw[:].bitcast(I32), in_=w3_words[0].bitcast(I32))
-        load_scale_rows(w3s_raw, w3_scales)
+        load_scale_rows(w3s_raw, w3_scales, [nc.sync] * 4)
 
-        def gather(window, lst, dtype, name):
-            got = sb([P, S], dtype, name)
+        def gather(window, lst, dtype, name, tag=""):
+            got = sb([P, S], dtype, name, tag)
             nc.vector.tensor_copy(got[:], window[:].indirect(lst[:]))
             return got
 
@@ -93,8 +95,8 @@ def tile_picked_twopage_none_po_kernel(
             )
             return dealt
 
-        def deal_scales(raw, name):
-            dealt = sb([P, H], U8, name)
+        def deal_scales(raw, name, tag=""):
+            dealt = sb([P, H], U8, name, tag)
             nc.vector.tensor_copy(
                 out=dealt[:].rearrange("p (t m) -> p t m", t=PACK),
                 in_=raw[:].rearrange("p (m t) -> p t m", t=PACK),
@@ -102,11 +104,12 @@ def tile_picked_twopage_none_po_kernel(
             return dealt
 
         x2s = gather(xs, two_t, U8, "x2s")
+        x1s = gather(xs, offs_t, U8, "x1s")
         x2w = gather(xw, two_t, U32, "x2w")
         w2w = deal_words(w2w_raw, "w2w")
+        w3w = deal_words(w3w_raw, "w3w")
         w2s = deal_scales(w2s_raw, "w2s")
-        x1w = gather(xw, offs_t, U32, "x1w")
-        x1s = gather(xs, offs_t, U8, "x1s")
+        x1w = gather(xw, offs_t, U32, "x1w", "w2s_raw")
 
         def product(lhsT, lhsT_scale, xw_t, xs_t, name):
             acc = psum.tile([P, S], F32, name="acc")
@@ -128,39 +131,41 @@ def tile_picked_twopage_none_po_kernel(
             out=w1b[:].rearrange("p (t m j) -> p m j t", t=PACK, j=PACK),
             in_=w1_raw[:].rearrange("p j (m t) -> p m j t", t=PACK),
         )
-        w1w = sb([P, H], U32, "w1w")
         w1s = sb([P, H], U8, "w1s")
-        nc.vector.tensor_copy(pb[0][:].indirect(s2_t[:]), e[0][:])
-        nc.vector.quantize_mx(out=w1w[:].bitcast(FP8X4), scales=w1s[:], in_=w1b[:])
-        y = [
-            product(w1w[:, P * t : P * (t + 1)].bitcast(FP8X4), w1s[:, P * t : P * (t + 1)], x1w, x1s, "y%d" % t)
-            for t in range(PACK)
-        ]
-        w3w = deal_words(w3w_raw, "w3w")
 
         gate = [sb([P, PACK, CH], F32, "gate%d" % c) for c in range(NCH)]
         read = [sb([P, PACK, CH], F32, "read%d" % c) for c in range(NCH)]
 
-        def fetch(dst, page, lst, t, func):
-            for c in range(NCH):
-                cols = slice(c * CH // 16, (c + 1) * CH // 16)
-                nc.scalar.activation(out=dst[c][:, t, :], in_=page[:].indirect(lst[:, cols]), func=func)
+        def fetch(dst, page, lst, t, func, n=CH):
+            for v0 in range(0, V, n):
+                c, lo = divmod(v0, CH)
+                nc.scalar.activation(
+                    out=dst[c][:, t, lo : lo + n], in_=page[:].indirect(lst[:, v0 // 16 : (v0 + n) // 16]), func=func
+                )
 
         for t in range(PACK):
-            if t > 0:
-                nc.vector.tensor_copy(pb[t][:].indirect(s2_t[:]), e[t][:])
+            nc.vector.tensor_copy(pb[t][:].indirect(s2_t[:]), e[t][:])
             fetch(gate, pb[t], r2_t, t, ACT.Sigmoid)
+            if t == 1:
+                w1w = sb([P, H], U32, "w1w", "e1")
+                nc.vector.quantize_mx(out=w1w[:].bitcast(FP8X4), scales=w1s[:], in_=w1b[:])
+                y = [
+                    product(w1w[:, P * u : P * (u + 1)].bitcast(FP8X4), w1s[:, P * u : P * (u + 1)], x1w, x1s, "y%d" % u)
+                    for u in range(PACK)
+                ]
         for t in range(PACK):
             nc.vector.tensor_copy(pa[t][:].indirect(s1_t[:]), y[t][:])
-            fetch(read, pa[t], r1_t, t, ACT.Copy)
-        w3s = deal_scales(w3s_raw, "w3s")
+            fetch(read, pa[t], r1_t, t, ACT.Copy, CH // 2 if t == PACK - 1 else CH)
+        w3s = deal_scales(w3s_raw, "w3s", "y3")
 
-        zb = [sb([P, PACK * CH], BF16, "zb%d" % c) for c in range(NCH)]
-        zw = [sb([P, CH], U32, "zw%d" % c) for c in range(NCH)]
-        zs = [sb([P, CH], U8, "zs%d" % c) for c in range(NCH)]
-        of = [sb([P, PACK, CH], F32, "of%d" % c) for c in range(NCH)]
-        ob = [sb([P, PACK * CH], BF16, "ob%d" % c) for c in range(NCH)]
-        ow = [sb([P, CH], U32, "ow%d" % c) for c in range(NCH)]
+        starts = [sum(WIDTHS[:k]) for k in range(len(WIDTHS))]
+        pieces = range(len(WIDTHS))
+        zb = [sb([P, PACK * WIDTHS[k]], BF16, "zb%d" % k) for k in pieces]
+        zw = [sb([P, WIDTHS[k]], U32, "zw%d" % k) for k in pieces]
+        zs = [sb([P, WIDTHS[k]], U8, "zs%d" % k) for k in pieces]
+        of = [sb([P, PACK, WIDTHS[k]], F32, "of%d" % k) for k in pieces]
+        ob = [sb([P, PACK * WIDTHS[k]], BF16, "ob%d" % k) for k in pieces]
+        ow = sb([P, V], U32, "ow")
         osc = sb([P, V], U8, "osc")
         out_rows = out_0.rearrange("(p t) v -> p t v", t=PACK)
         out_words = out_1[0].rearrange("p c r -> p (c r)").bitcast(I32)
@@ -171,46 +176,53 @@ def tile_picked_twopage_none_po_kernel(
         def woven(ap):
             return ap.rearrange("p (c i t) -> p c t i", i=4, t=PACK)
 
-        def mult(c):
-            nc.vector.tensor_tensor(woven(zb[c][:]), planes(read[c][:]), planes(gate[c][:]), MULT)
+        def mult(k):
+            c, lo = divmod(starts[k], CH)
+            cols = slice(lo, lo + WIDTHS[k])
+            nc.vector.tensor_tensor(woven(zb[k][:]), planes(read[c][:, :, cols]), planes(gate[c][:, :, cols]), MULT)
 
-        def quant_z(c):
-            nc.vector.quantize_mx(out=zw[c][:].bitcast(FP8X4), scales=zs[c][:], in_=zb[c][:])
-
-        def last_product(c):
-            for h in range(2):
+        def quant_z(k):
+            nc.vector.quantize_mx(out=zw[k][:].bitcast(FP8X4), scales=zs[k][:], in_=zb[k][:])
+            w = WIDTHS[k]
+            per_bank = S // w
+            for t0 in range(0, PACK, per_bank):
                 acc = psum.tile([P, S], F32, name="acc")
-                for u in range(2):
-                    t = 2 * h + u
+                for u in range(per_bank):
+                    t = t0 + u
                     nc.tensor.matmul_mx(
-                        out=acc[:, u * CH : (u + 1) * CH],
+                        out=acc[:, u * w : (u + 1) * w],
                         lhsT=w3w[:, 2 * P * t : 2 * P * (t + 1)].bitcast(FP4X4),
                         lhsT_scale=w3s[:, P * t : P * (t + 1)],
-                        rhs=zw[c][:].bitcast(FP8X4), rhs_scale=zs[c][:], start=True, stop=True,
+                        rhs=zw[k][:].bitcast(FP8X4), rhs_scale=zs[k][:], start=True, stop=True,
                     )
-                nc.scalar.copy(out=of[c][:, 2 * h : 2 * h + 2, :].rearrange("p t c -> p (t c)"), in_=acc[:])
-            nc.sync.dma_start(out=out_rows[:, :, c * CH : (c + 1) * CH], in_=of[c][:])
+                nc.scalar.copy(out=of[k][:, t0 : t0 + per_bank, :].rearrange("p t c -> p (t c)"), in_=acc[:])
+            nc.sync.dma_start(out=out_rows[:, :, starts[k] : starts[k] + w], in_=of[k][:])
+            if k in ROUND_ON_SCALAR:
+                nc.scalar.copy(out=woven(ob[k][:]), in_=planes(of[k][:]))
 
-        def round_out(c):
-            nc.vector.tensor_copy(out=woven(ob[c][:]), in_=planes(of[c][:]))
+        def round_out(k):
+            if k not in ROUND_ON_SCALAR:
+                nc.vector.tensor_copy(out=woven(ob[k][:]), in_=planes(of[k][:]))
 
-        def quant_out(c):
-            cols = slice(c * CH, (c + 1) * CH)
-            nc.vector.quantize_mx(out=ow[c][:].bitcast(FP8X4), scales=osc[:, cols], in_=ob[c][:])
-            nc.sync.dma_start(out=out_words[:, cols], in_=ow[c][:].bitcast(I32))
+        def quant_out(k):
+            cols = slice(starts[k], starts[k] + WIDTHS[k])
+            nc.vector.quantize_mx(out=ow[:, cols].bitcast(FP8X4), scales=osc[:, cols], in_=ob[k][:])
+            if cols.stop % (V // 2) == 0:
+                half = slice(cols.stop - V // 2, cols.stop)
+                nc.sync.dma_start(out=out_words[:, half], in_=ow[:, half].bitcast(I32))
 
-        for step in range(NCH + 3):
-            if step < NCH:
-                mult(step)
-            if 1 <= step <= NCH:
-                quant_z(step - 1)
-                last_product(step - 1)
-            if 3 <= step:
-                quant_out(step - 3)
-            if 2 <= step < NCH + 2:
-                round_out(step - 2)
+        for k in range(len(WIDTHS) + 1):
+            if k < len(WIDTHS):
+                mult(k)
+            if k >= 1:
+                quant_z(k - 1)
+        for k in range(len(WIDTHS) + 1):
+            if k < len(WIDTHS):
+                round_out(k)
+            if k >= 1:
+                quant_out(k - 1)
         for q in range(4):
-            nc.sync.dma_start(
+            (nc.sync if q % 2 else nc.scalar).dma_start(
                 out=out_2[0, 4 * q : 4 * q + 4, :].bitcast(I32),
                 in_=osc[32 * q : 32 * q + 4, :].bitcast(I32),
             )

from contextlib import ExitStack

import concourse.mybir as mybir

K, T, S, V, N, U, H = 512, 2048, 512, 1024, 512, 1024, 512
FLOPS = 2 * K * H * S * 2 + 2 * H * N * V

F32 = mybir.dt.float32
BF16 = mybir.dt.bfloat16
I32 = mybir.dt.int32
U32 = mybir.dt.uint32
U16 = mybir.dt.uint16
U8 = mybir.dt.uint8
FP8X4 = mybir.dt.float8_e4m3fn_x4
FP4X4 = mybir.dt.float4_e2m1fn_x4
ACT = mybir.ActivationFunctionType
MULT = mybir.AluOpType.mult

P = 128
PACK = 4
CH = 512
NCH = V // CH
WIDTHS = (128, 128, 256, 256, 256)
ROUND_ON_SCALAR = (0, 1)


def tile_picked_twopage_none_po_kernel(
    tc, x_words, x_scales, w1, w2_words, w2_scales, ma, mb, w3_words, w3_scales,
    offs, two, s1, s2, r1, r2, out_0, out_1, out_2,
):
    nc = tc.nc
    with ExitStack() as ctx:
        keep = ctx.enter_context(tc.tile_pool(name="keep", bufs=1))
        psum = ctx.enter_context(tc.psum_pool(name="psum", bufs=8))

        def sb(shape, dtype, name, tag=""):
            return keep.tile(shape, dtype, name=name, tag=tag or name, align_bytes=64)

        def load_list(src, name):
            t = sb([P, src.shape[1]], U16, name)
            nc.sync.dma_start(t[:], src)
            return t

        def load_scale_rows(tile, src, queues):
            for q in range(4):
                queues[q].dma_start(
                    out=tile[32 * q : 32 * q + 4, :].bitcast(I32),
                    in_=src[0, 4 * q : 4 * q + 4, :].bitcast(I32),
                )

        def load_page(src, t, name):
            page = sb([P, U], F32, name)
            nc.sync.dma_start(out=page[:], in_=src.rearrange("(p t) u -> p t u", t=PACK)[:, t, :])
            return page

        xs = sb([P, T], U8, "xs")
        w2s_raw = sb([P, H], U8, "w2s_raw")
        w3s_raw = sb([P, N], U8, "w3s_raw")
        nc.vector.memset(xs[:].bitcast(I32), 0)
        nc.vector.memset(w2s_raw[:].bitcast(I32), 0)
        nc.vector.memset(w3s_raw[:].bitcast(I32), 0)

        two_t = load_list(two, "two_t")
        offs_t = load_list(offs, "offs_t")
        w2w_raw = sb([P, 2 * H], U8, "w2w_raw")
        nc.sync.dma_start(out=w2w_raw[:].bitcast(I32), in_=w2_words[0].bitcast(I32))
        load_scale_rows(xs, x_scales, [nc.sync] * 4)
        xw = sb([P, T], U32, "xw")
        nc.sync.dma_start(out=xw[:].bitcast(I32), in_=x_words[0].rearrange("p c r -> p (c r)").bitcast(I32))
        load_scale_rows(w2s_raw, w2_scales, [nc.sync] * 4)
        w3w_raw = sb([P, 2 * N], U8, "w3w_raw")
        nc.sync.dma_start(out=w3w_raw[:].bitcast(I32), in_=w3_words[0].bitcast(I32))
        s2_t = load_list(s2, "s2_t")
        pb = [load_page(mb, 0, "pb0")]
        w1_raw = sb([P, PACK, H], F32, "w1_raw")
        nc.sync.dma_start(out=w1_raw[:], in_=w1.rearrange("(p j) c -> p j c", j=PACK))
        r2_t = load_list(r2, "r2_t")
        s1_t = load_list(s1, "s1_t")
        r1_t = load_list(r1, "r1_t")
        for t in range(1, PACK):
            pb.append(load_page(mb, t, "pb%d" % t))
        pa = [load_page(ma, t, "pa%d" % t) for t in range(PACK)]
        load_scale_rows(w3s_raw, w3_scales, [nc.sync] * 4)

        def gather(window, lst, dtype, name, tag=""):
            got = sb([P, S], dtype, name, tag)
            nc.vector.tensor_copy(got[:], window[:].indirect(lst[:]))
            return got

        def deal_words(raw, name):
            dealt = sb([P, 2 * H], U8, name)
            nc.scalar.copy(
                out=dealt[:].bitcast(U16).rearrange("p (t m) -> p m t", t=PACK),
                in_=raw[:].bitcast(U16).rearrange("p (m t) -> p m t", t=PACK),
            )
            return dealt

        def deal_scales(raw, name, tag=""):
            dealt = sb([P, H], U8, name, tag)
            nc.vector.tensor_copy(
                out=dealt[:].rearrange("p (t m) -> p t m", t=PACK),
                in_=raw[:].rearrange("p (m t) -> p t m", t=PACK),
            )
            return dealt

        x2s = gather(xs, two_t, U8, "x2s")
        x1s = gather(xs, offs_t, U8, "x1s")
        x2w = gather(xw, two_t, U32, "x2w")
        w2w = deal_words(w2w_raw, "w2w")
        w3w = deal_words(w3w_raw, "w3w")
        w2s = deal_scales(w2s_raw, "w2s")
        x1w = gather(xw, offs_t, U32, "x1w", "w2s_raw")

        def product(lhsT, lhsT_scale, xw_t, xs_t, name):
            acc = psum.tile([P, S], F32, name="acc")
            nc.tensor.matmul_mx(
                out=acc[:], lhsT=lhsT, lhsT_scale=lhsT_scale,
                rhs=xw_t[:].bitcast(FP8X4), rhs_scale=xs_t[:], start=True, stop=True,
            )
            res = sb([P, S], F32, name)
            nc.scalar.copy(out=res[:], in_=acc[:])
            return res

        e = [
            product(w2w[:, 2 * P * t : 2 * P * (t + 1)].bitcast(FP4X4), w2s[:, P * t : P * (t + 1)], x2w, x2s, "e%d" % t)
            for t in range(PACK)
        ]

        w1b = sb([P, PACK * H], BF16, "w1b")
        nc.scalar.copy(
            out=w1b[:].rearrange("p (t m j) -> p m j t", t=PACK, j=PACK),
            in_=w1_raw[:].rearrange("p j (m t) -> p m j t", t=PACK),
        )
        w1s = sb([P, H], U8, "w1s")

        gate = [sb([P, PACK, CH], F32, "gate%d" % c) for c in range(NCH)]
        read = [sb([P, PACK, CH], F32, "read%d" % c) for c in range(NCH)]

        def fetch(dst, page, lst, t, func, n=CH):
            for v0 in range(0, V, n):
                c, lo = divmod(v0, CH)
                nc.scalar.activation(
                    out=dst[c][:, t, lo : lo + n], in_=page[:].indirect(lst[:, v0 // 16 : (v0 + n) // 16]), func=func
                )

        for t in range(PACK):
            nc.vector.tensor_copy(pb[t][:].indirect(s2_t[:]), e[t][:])
            fetch(gate, pb[t], r2_t, t, ACT.Sigmoid)
            if t == 1:
                w1w = sb([P, H], U32, "w1w", "e1")
                nc.vector.quantize_mx(out=w1w[:].bitcast(FP8X4), scales=w1s[:], in_=w1b[:])
                y = [
                    product(w1w[:, P * u : P * (u + 1)].bitcast(FP8X4), w1s[:, P * u : P * (u + 1)], x1w, x1s, "y%d" % u)
                    for u in range(PACK)
                ]
        for t in range(PACK):
            nc.vector.tensor_copy(pa[t][:].indirect(s1_t[:]), y[t][:])
            fetch(read, pa[t], r1_t, t, ACT.Copy, CH // 2 if t == PACK - 1 else CH)
        w3s = deal_scales(w3s_raw, "w3s", "y3")

        starts = [sum(WIDTHS[:k]) for k in range(len(WIDTHS))]
        pieces = range(len(WIDTHS))
        zb = [sb([P, PACK * WIDTHS[k]], BF16, "zb%d" % k) for k in pieces]
        zw = [sb([P, WIDTHS[k]], U32, "zw%d" % k) for k in pieces]
        zs = [sb([P, WIDTHS[k]], U8, "zs%d" % k) for k in pieces]
        of = [sb([P, PACK, WIDTHS[k]], F32, "of%d" % k) for k in pieces]
        ob = [sb([P, PACK * WIDTHS[k]], BF16, "ob%d" % k) for k in pieces]
        ow = sb([P, V], U32, "ow")
        osc = sb([P, V], U8, "osc")
        out_rows = out_0.rearrange("(p t) v -> p t v", t=PACK)
        out_words = out_1[0].rearrange("p c r -> p (c r)").bitcast(I32)

        def planes(ap):
            return ap.rearrange("p t (c i) -> p c t i", i=4)

        def woven(ap):
            return ap.rearrange("p (c i t) -> p c t i", i=4, t=PACK)

        def mult(k):
            c, lo = divmod(starts[k], CH)
            cols = slice(lo, lo + WIDTHS[k])
            nc.vector.tensor_tensor(woven(zb[k][:]), planes(read[c][:, :, cols]), planes(gate[c][:, :, cols]), MULT)

        def quant_z(k):
            nc.vector.quantize_mx(out=zw[k][:].bitcast(FP8X4), scales=zs[k][:], in_=zb[k][:])
            w = WIDTHS[k]
            per_bank = S // w
            for t0 in range(0, PACK, per_bank):
                acc = psum.tile([P, S], F32, name="acc")
                for u in range(per_bank):
                    t = t0 + u
                    nc.tensor.matmul_mx(
                        out=acc[:, u * w : (u + 1) * w],
                        lhsT=w3w[:, 2 * P * t : 2 * P * (t + 1)].bitcast(FP4X4),
                        lhsT_scale=w3s[:, P * t : P * (t + 1)],
                        rhs=zw[k][:].bitcast(FP8X4), rhs_scale=zs[k][:], start=True, stop=True,
                    )
                nc.scalar.copy(out=of[k][:, t0 : t0 + per_bank, :].rearrange("p t c -> p (t c)"), in_=acc[:])
            nc.sync.dma_start(out=out_rows[:, :, starts[k] : starts[k] + w], in_=of[k][:])
            if k in ROUND_ON_SCALAR:
                nc.scalar.copy(out=woven(ob[k][:]), in_=planes(of[k][:]))

        def round_out(k):
            if k not in ROUND_ON_SCALAR:
                nc.vector.tensor_copy(out=woven(ob[k][:]), in_=planes(of[k][:]))

        def quant_out(k):
            cols = slice(starts[k], starts[k] + WIDTHS[k])
            nc.vector.quantize_mx(out=ow[:, cols].bitcast(FP8X4), scales=osc[:, cols], in_=ob[k][:])
            if cols.stop % (V // 2) == 0:
                half = slice(cols.stop - V // 2, cols.stop)
                nc.sync.dma_start(out=out_words[:, half], in_=ow[:, half].bitcast(I32))

        for k in range(len(WIDTHS) + 1):
            if k < len(WIDTHS):
                mult(k)
            if k >= 1:
                quant_z(k - 1)
        for k in range(len(WIDTHS) + 1):
            if k < len(WIDTHS):
                round_out(k)
            if k >= 1:
                quant_out(k - 1)
        for q in range(4):
            (nc.sync if q % 2 else nc.scalar).dma_start(
                out=out_2[0, 4 * q : 4 * q + 4, :].bitcast(I32),
                in_=osc[32 * q : 32 * q + 4, :].bitcast(I32),
            )
